import numpy as np
import ml_dtypes


def mxq(x, axis, fmt="e4m3"):
    dtype, down = {"e4m3": (ml_dtypes.float8_e4m3fn, 7), "e5m2": (ml_dtypes.float8_e5m2, 14)}[fmt]
    v = np.moveaxis(np.asarray(x, np.float32).astype(ml_dtypes.bfloat16).astype(np.float64), axis, -1)
    blocks = v.reshape(v.shape[:-1] + (-1, 32))
    amax = np.abs(blocks).max(-1, keepdims=True)
    byte = np.maximum(np.where(amax > 0, np.frexp(amax)[1] - 1 + 127, 0) - down, 1)
    scale = np.exp2(byte - 127.0)
    codes = (blocks / scale).astype(np.float32).astype(dtype).astype(np.float64)
    return np.moveaxis((codes * scale).reshape(v.shape), -1, axis)


WIDE = False


def mx_kscale(k):
    if not WIDE:
        return np.ones(k)
    levels = np.array([10, -10, 5, -5, 0])
    if k % 512:
        return np.exp2(np.random.permutation(np.resize(levels, k // 32))).repeat(32)
    a = np.empty((k // 512, 16))
    for p in range(k // 512):
        a[p, :8] = np.random.permutation(np.resize(levels, 8))
        for g in range(8):
            far = levels[np.abs(levels - a[p, g]) >= 10]
            a[p, g + 8] = far[np.random.randint(len(far))]
    return np.exp2(a.ravel()).repeat(32)


def f64(x):
    return np.asarray(x).astype(np.float64)


E2M1 = np.array([0.0, 0.5, 1.0, 1.5, 2.0, 3.0, 4.0, 6.0, -0.0, -0.5, -1.0, -1.5, -2.0, -3.0, -4.0, -6.0])


def pack_weight(w, fmt):
    k, n = w.shape
    w = f64(np.asarray(w, np.float32).astype(ml_dtypes.bfloat16)).reshape(k // 32, 32, n)
    amax = np.abs(w).max(1)
    if fmt == "e4m3":
        byte = np.frexp(amax)[1] - 1 + 127 - 7
    else:
        mant, ex = np.frexp(amax / 6.0)
        byte = np.where(mant > 0.5, ex, ex - 1) + 127
    byte = np.clip(np.where(amax > 0, byte, 1), 1, 254)
    scaled = (w * np.exp2(127.0 - byte)[:, None, :]).reshape(k, n).astype(np.float32)
    by_word = np.ascontiguousarray(scaled.reshape(k // 512, 128, 4, n).transpose(0, 1, 3, 2))
    if fmt == "e4m3":
        words = by_word.astype(ml_dtypes.float8_e4m3fn).view(np.uint8)
    else:
        c = by_word.astype(ml_dtypes.float4_e2m1fn).view(np.uint8) & 0xF
        words = (c[..., 0::2] | (c[..., 1::2] << 4)).reshape(k // 512, 128, 2 * n)
    return np.ascontiguousarray(words), np.ascontiguousarray(byte.astype(np.uint8).reshape(k // 512, 16, n))


def unpack_weight(words, scales, fmt):
    g, _, n = scales.shape
    words = np.ascontiguousarray(words).reshape(g, 128, n, -1)
    if fmt == "e4m3":
        vals = words.view(ml_dtypes.float8_e4m3fn).astype(np.float64)
    else:
        nib = np.empty((g, 128, n, 4), np.uint8)
        nib[..., 0::2] = words & 0xF
        nib[..., 1::2] = words >> 4
        vals = E2M1[nib]
    vals = vals * np.repeat(np.exp2(scales.astype(np.float64) - 127.0), 8, axis=1)[..., None]
    return vals.transpose(0, 1, 3, 2).reshape(g * 512, n)


def silu(v):
    return v / (1.0 + np.exp(-np.maximum(v, -700.0)))


K, M, T = 1536, 1024, 1536


def setup_inputs():
    n = np.random.standard_normal
    s = mx_kscale(K)[:, None]
    w = n((K, M)) / np.sqrt(K) / s
    w4 = pack_weight(w, "e2m1")
    rest = w - unpack_weight(*w4, "e2m1")
    p_r8 = pack_weight(rest, "e4m3")
    return {
        "x": (n((K, T)) * s).astype(np.float32),
        "w4_words": w4[0],
        "w4_scales": w4[1],
        "r8_words": p_r8[0],
        "r8_scales": p_r8[1],
        "b": (0.3 * n(1024)).astype(np.float32),
    }


def reference(x, w4_words, w4_scales, r8_words, r8_scales, b):
    x_ = mxq(f64(x), 0, "e4m3")
    w4_ = unpack_weight(w4_words, w4_scales, "e2m1")
    r8_ = unpack_weight(r8_words, r8_scales, "e4m3")
    y = w4_.T @ x_ + r8_.T @ x_
    return silu(y + f64(b)[:, None])

@@ -1,0 +1,194 @@
+from contextlib import ExitStack
+
+import concourse.mybir as mybir
+
+K, M, T = 1536, 1024, 1536
+FLOPS = 2 * 2 * K * M * T
+
+F32 = mybir.dt.float32
+BF16 = mybir.dt.bfloat16
+I32 = mybir.dt.int32
+U32 = mybir.dt.uint32
+U8 = mybir.dt.uint8
+FP8X4 = mybir.dt.float8_e4m3fn_x4
+FP4X4 = mybir.dt.float4_e2m1fn_x4
+ACT = mybir.ActivationFunctionType
+
+P = 128
+PACK = 4
+G = K // 512
+MT = M // 128
+TW = 512
+NT = T // TW
+HALF = 256
+V_COLS = 160
+
+
+def tile_mix_resid_fm_silu_kernel(tc, x, w4_words, w4_scales, r8_words, r8_scales, b, out):
+    nc = tc.nc
+    with ExitStack() as ctx:
+        keep = ctx.enter_context(tc.tile_pool(name="keep", bufs=1))
+        stage = ctx.enter_context(tc.tile_pool(name="stage", bufs=6))
+        outs = ctx.enter_context(tc.tile_pool(name="outs", bufs=24))
+        psum = ctx.enter_context(tc.psum_pool(name="psum", bufs=1))
+        ctx.enter_context(tc.manual_schedule())
+
+        raw = {}
+        codes = {}
+        planes = {}
+        for t in range(NT):
+            for g in range(G):
+                raw[g, t] = keep.tile([P, PACK, TW], F32, name="raw_%d_%d" % (g, t), align_bytes=64)
+                codes[g, t] = keep.tile([P, TW], U32, name="codes_%d_%d" % (g, t), align_bytes=256)
+                planes[g, t] = keep.tile([P, TW], U8, name="plane_%d_%d" % (g, t), align_bytes=256)
+        w4 = [keep.tile([P, 2 * M], U8, name="w4_%d" % g, align_bytes=256) for g in range(G)]
+        r8 = [keep.tile([P, 4 * M], U8, name="r8_%d" % g, align_bytes=256) for g in range(G)]
+        w4s = keep.tile([P, G, M], U8, name="w4s", align_bytes=256)
+        r8s = keep.tile([P, G, M], U8, name="r8s", align_bytes=256)
+        b_rows = keep.tile([P, 32], F32, name="b_rows", align_bytes=64)
+        b_cols = keep.tile([P, 32], F32, name="b_cols", align_bytes=64)
+        warm = keep.tile([P, 1], F32, name="warm")
+        warm_out = keep.tile([P, 1], F32, name="warm_out")
+
+        w4s_i = w4s[:].rearrange("p g n -> p (g n)").bitcast(I32)
+        r8s_i = r8s[:].rearrange("p g n -> p (g n)").bitcast(I32)
+        nc.vector.memset(w4s_i, 0)
+        nc.vector.memset(warm[:], 0.0)
+        nc.gpsimd.memset(r8s_i, 0)
+        nc.gpsimd.memset(b_rows[:], 0.0)
+
+        def load_x(g, t, c0, c1):
+            nc.sync.dma_start(
+                out=raw[g, t][:, :, c0:c1],
+                in_=x[512 * g : 512 * (g + 1), TW * t + c0 : TW * t + c1].rearrange("(p j) t -> p j t", j=PACK),
+            )
+
+        def load_w4(g):
+            nc.sync.dma_start(out=w4[g][:].bitcast(I32), in_=w4_words[g].bitcast(I32))
+
+        def load_r8(g):
+            nc.sync.dma_start(out=r8[g][:].bitcast(I32), in_=r8_words[g].rearrange("p n i -> p (n i)").bitcast(I32))
+
+        def load_scales(queue, view, scales, q):
+            queue.dma_start(
+                out=view[32 * q : 32 * q + 4, :].rearrange("p (g n) -> p g n", g=G),
+                in_=scales.bitcast(I32)[:, 4 * q : 4 * q + 4, :].rearrange("g r n -> r g n"),
+            )
+
+        load_x(0, 0, 0, HALF)
+        load_x(0, 0, HALF, TW)
+        for q in range(4):
+            load_scales(nc.scalar, w4s_i, w4_scales, q)
+        for q in range(4):
+            load_scales(nc.gpsimd, r8s_i, r8_scales, q)
+        for q in range(4):
+            nc.gpsimd.dma_start(
+                out=b_rows[32 * q : 32 * q + 8, :],
+                in_=b.rearrange("(m q j) -> q m j", q=4, j=32)[q],
+            )
+        nc.scalar.activation(out=warm_out[:], in_=warm[:], func=ACT.Silu)
+        load_w4(0)
+        load_r8(0)
+        for g in range(1, G):
+            load_x(g, 0, 0, TW)
+            load_w4(g)
+            load_r8(g)
+        for t in range(1, NT):
+            for g in range(G):
+                load_x(g, t, 0, TW)
+
+        def cast(g, t, h, v_cols):
+            grouped = stage.tile([P, HALF, PACK], BF16, name="grouped", align_bytes=64)
+            c0 = h * HALF
+            nc.vector.tensor_copy(
+                out=grouped[:, :v_cols, :], in_=raw[g, t][:, :, c0 : c0 + v_cols].rearrange("p j w -> p w j")
+            )
+            if v_cols < HALF:
+                nc.scalar.copy(
+                    out=grouped[:, v_cols:, :],
+                    in_=raw[g, t][:, :, c0 + v_cols : c0 + HALF].rearrange("p j w -> p w j"),
+                )
+            return grouped
+
+        def quantise(g, t, h, grouped):
+            cols = slice(h * HALF, (h + 1) * HALF)
+            nc.vector.quantize_mx(
+                out=codes[g, t][:, cols].bitcast(FP8X4),
+                scales=planes[g, t][:, cols],
+                in_=grouped[:].rearrange("p w j -> p (w j)"),
+            )
+
+        acc = {}
+
+        def mm_w4(m, g, t):
+            if g == 0:
+                acc[m] = psum.tile([P, TW], F32, name="bank%d" % m)
+            nc.tensor.matmul_mx(
+                out=acc[m][:],
+                lhsT=w4[g][:, 256 * m : 256 * (m + 1)].bitcast(FP4X4),
+                lhsT_scale=w4s[:, g, P * m : P * (m + 1)],
+                rhs=codes[g, t][:].bitcast(FP8X4),
+                rhs_scale=planes[g, t][:],
+                start=(g == 0),
+                stop=False,
+            )
+
+        def mm_r8(m, g, t):
+            nc.tensor.matmul_mx(
+                out=acc[m][:],
+                lhsT=r8[g][:, 512 * m : 512 * (m + 1)].bitcast(FP8X4),
+                lhsT_scale=r8s[:, g, P * m : P * (m + 1)],
+                rhs=codes[g, t][:].bitcast(FP8X4),
+                rhs_scale=planes[g, t][:],
+                start=False,
+                stop=(g == G - 1),
+            )
+
+        def finish(m, t, pieces):
+            width = TW // pieces
+            res = outs.tile([P, TW], F32, name="res")
+            for i in range(pieces):
+                cols = slice(i * width, (i + 1) * width)
+                nc.scalar.activation(out=res[:, cols], in_=acc[m][:, cols], func=ACT.Silu, bias=b_cols[:, m : m + 1])
+                nc.sync.dma_start(
+                    out=out[P * m : P * (m + 1), TW * t + i * width : TW * t + (i + 1) * width], in_=res[:, cols]
+                )
+
+        for h in range(2):
+            grouped = cast(0, 0, h, V_COLS)
+            quantise(0, 0, h, grouped)
+        for m in range(MT):
+            mm_w4(m, 0, 0)
+        for m in range(MT):
+            mm_r8(m, 0, 0)
+
+        def chunk(g, t, v_cols):
+            halves = [cast(g, t, h, v_cols) for h in range(2)]
+            for h in range(2):
+                quantise(g, t, h, halves[h])
+
+        for g in range(1, G):
+            chunk(g, 0, V_COLS)
+            if g == 1:
+                nc.vector.transpose(out=b_cols[:], in_=b_rows[:])
+            for m in range(MT):
+                mm_w4(m, g, 0)
+                mm_r8(m, g, 0)
+                if g == G - 1:
+                    finish(m, 0, 1)
+
+        for g in range(G):
+            chunk(g, 1, HALF)
+        for g in range(G):
+            chunk(g, 2, HALF)
+        for g in range(G):
+            for m in range(MT):
+                mm_w4(m, g, 1)
+                mm_r8(m, g, 1)
+                if g == G - 1:
+                    finish(m, 1, 1)
+        for m in range(MT):
+            for g in range(G):
+                mm_w4(m, g, 2)
+                mm_r8(m, g, 2)
+            finish(m, 2, 2 if m == MT - 1 else 1)

@@ -29,7 +29,7 @@ def tile_mix_resid_fm_silu_kernel(tc, x, w4_words, w4_scales, r8_words, r8_scale
     with ExitStack() as ctx:
         keep = ctx.enter_context(tc.tile_pool(name="keep", bufs=1))
         stage = ctx.enter_context(tc.tile_pool(name="stage", bufs=6))
-        outs = ctx.enter_context(tc.tile_pool(name="outs", bufs=24))
+        outs = ctx.enter_context(tc.tile_pool(name="outs", bufs=26))
         psum = ctx.enter_context(tc.psum_pool(name="psum", bufs=1))
         ctx.enter_context(tc.manual_schedule())
 
@@ -79,116 +79,120 @@ def tile_mix_resid_fm_silu_kernel(tc, x, w4_words, w4_scales, r8_words, r8_scale
         load_x(0, 0, HALF, TW)
         for q in range(4):
             load_scales(nc.scalar, w4s_i, w4_scales, q)
-        for q in range(4):
-            load_scales(nc.gpsimd, r8s_i, r8_scales, q)
-        for q in range(4):
-            nc.gpsimd.dma_start(
-                out=b_rows[32 * q : 32 * q + 8, :],
-                in_=b.rearrange("(m q j) -> q m j", q=4, j=32)[q],
-            )
         nc.scalar.activation(out=warm_out[:], in_=warm[:], func=ACT.Silu)
         load_w4(0)
+        for q in range(4):
+            load_scales(nc.sync, r8s_i, r8_scales, q)
         load_r8(0)
         for g in range(1, G):
             load_x(g, 0, 0, TW)
             load_w4(g)
+            if g == 1:
+                for q in range(4):
+                    nc.sync.dma_start(
+                        out=b_rows[32 * q : 32 * q + 8, :],
+                        in_=b.rearrange("(m q j) -> q m j", q=4, j=32)[q],
+                    )
             load_r8(g)
         for t in range(1, NT):
             for g in range(G):
                 load_x(g, t, 0, TW)
 
-        def cast(g, t, h, v_cols):
+        def cast(g, t, c0, width, v_cols):
             grouped = stage.tile([P, HALF, PACK], BF16, name="grouped", align_bytes=64)
-            c0 = h * HALF
             nc.vector.tensor_copy(
                 out=grouped[:, :v_cols, :], in_=raw[g, t][:, :, c0 : c0 + v_cols].rearrange("p j w -> p w j")
             )
-            if v_cols < HALF:
+            if v_cols < width:
                 nc.scalar.copy(
-                    out=grouped[:, v_cols:, :],
-                    in_=raw[g, t][:, :, c0 + v_cols : c0 + HALF].rearrange("p j w -> p w j"),
+                    out=grouped[:, v_cols:width, :],
+                    in_=raw[g, t][:, :, c0 + v_cols : c0 + width].rearrange("p j w -> p w j"),
                 )
             return grouped
 
-        def quantise(g, t, h, grouped):
-            cols = slice(h * HALF, (h + 1) * HALF)
+        def quantise(g, t, c0, width, grouped):
+            cols = slice(c0, c0 + width)
             nc.vector.quantize_mx(
                 out=codes[g, t][:, cols].bitcast(FP8X4),
                 scales=planes[g, t][:, cols],
-                in_=grouped[:].rearrange("p w j -> p (w j)"),
+                in_=grouped[:, :width, :].rearrange("p w j -> p (w j)"),
             )
 
         acc = {}
 
-        def mm_w4(m, g, t):
+        def mm_w4(m, g, t, c0=0, width=TW):
             if g == 0:
-                acc[m] = psum.tile([P, TW], F32, name="bank%d" % m)
+                acc[m] = psum.tile([P, TW], F32, name="bank%d" % ((m + c0 // P) % MT))
             nc.tensor.matmul_mx(
-                out=acc[m][:],
+                out=acc[m][:, :width],
                 lhsT=w4[g][:, 256 * m : 256 * (m + 1)].bitcast(FP4X4),
                 lhsT_scale=w4s[:, g, P * m : P * (m + 1)],
-                rhs=codes[g, t][:].bitcast(FP8X4),
-                rhs_scale=planes[g, t][:],
+                rhs=codes[g, t][:, c0 : c0 + width].bitcast(FP8X4),
+                rhs_scale=planes[g, t][:, c0 : c0 + width],
                 start=(g == 0),
                 stop=False,
             )
 
-        def mm_r8(m, g, t):
+        def mm_r8(m, g, t, c0=0, width=TW):
             nc.tensor.matmul_mx(
-                out=acc[m][:],
+                out=acc[m][:, :width],
                 lhsT=r8[g][:, 512 * m : 512 * (m + 1)].bitcast(FP8X4),
                 lhsT_scale=r8s[:, g, P * m : P * (m + 1)],
-                rhs=codes[g, t][:].bitcast(FP8X4),
-                rhs_scale=planes[g, t][:],
+                rhs=codes[g, t][:, c0 : c0 + width].bitcast(FP8X4),
+                rhs_scale=planes[g, t][:, c0 : c0 + width],
                 start=False,
                 stop=(g == G - 1),
             )
 
-        def finish(m, t, pieces):
-            width = TW // pieces
+        def finish(m, t, c0=0, width=TW):
             res = outs.tile([P, TW], F32, name="res")
-            for i in range(pieces):
-                cols = slice(i * width, (i + 1) * width)
-                nc.scalar.activation(out=res[:, cols], in_=acc[m][:, cols], func=ACT.Silu, bias=b_cols[:, m : m + 1])
-                nc.sync.dma_start(
-                    out=out[P * m : P * (m + 1), TW * t + i * width : TW * t + (i + 1) * width], in_=res[:, cols]
-                )
+            nc.scalar.activation(
+                out=res[:, :width], in_=acc[m][:, :width], func=ACT.Silu, bias=b_cols[:, m : m + 1]
+            )
+            nc.sync.dma_start(
+                out=out[P * m : P * (m + 1), TW * t + c0 : TW * t + c0 + width], in_=res[:, :width]
+            )
 
-        for h in range(2):
-            grouped = cast(0, 0, h, V_COLS)
-            quantise(0, 0, h, grouped)
+        def chunk(g, t, width, v_cols):
+            parts = [(c0, cast(g, t, c0, width, v_cols)) for c0 in range(0, TW, width)]
+            for c0, grouped in parts:
+                quantise(g, t, c0, width, grouped)
+
+        halves0 = cast(0, 0, 0, HALF, V_COLS)
+        quantise(0, 0, 0, HALF, halves0)
+        halves1 = cast(0, 0, 256, 128, 80)
+        halves2 = cast(0, 0, 384, 128, 80)
+        quantise(0, 0, 256, 128, halves1)
+        quantise(0, 0, 384, 128, halves2)
         for m in range(MT):
             mm_w4(m, 0, 0)
         for m in range(MT):
             mm_r8(m, 0, 0)
 
-        def chunk(g, t, v_cols):
-            halves = [cast(g, t, h, v_cols) for h in range(2)]
-            for h in range(2):
-                quantise(g, t, h, halves[h])
-
         for g in range(1, G):
-            chunk(g, 0, V_COLS)
-            if g == 1:
+            chunk(g, 0, HALF, V_COLS)
+            if g == 2:
                 nc.vector.transpose(out=b_cols[:], in_=b_rows[:])
             for m in range(MT):
                 mm_w4(m, g, 0)
                 mm_r8(m, g, 0)
                 if g == G - 1:
-                    finish(m, 0, 1)
+                    finish(m, 0)
 
         for g in range(G):
-            chunk(g, 1, HALF)
+            chunk(g, 1, HALF, HALF)
         for g in range(G):
-            chunk(g, 2, HALF)
+            chunk(g, 2, HALF, HALF)
         for g in range(G):
             for m in range(MT):
                 mm_w4(m, g, 1)
                 mm_r8(m, g, 1)
                 if g == G - 1:
-                    finish(m, 1, 1)
+                    finish(m, 1)
         for m in range(MT):
-            for g in range(G):
-                mm_w4(m, g, 2)
-                mm_r8(m, g, 2)
-            finish(m, 2, 2 if m == MT - 1 else 1)
+            width = 128 if m == MT - 1 else TW
+            for c0 in range(0, TW, width):
+                for g in range(G):
+                    mm_w4(m, g, 2, c0, width)
+                    mm_r8(m, g, 2, c0, width)
+                finish(m, 2, c0, width)

@@ -54,8 +54,8 @@ def tile_mix_resid_fm_silu_kernel(tc, x, w4_words, w4_scales, r8_words, r8_scale
         r8s_i = r8s[:].rearrange("p g n -> p (g n)").bitcast(I32)
         nc.vector.memset(w4s_i, 0)
         nc.vector.memset(warm[:], 0.0)
-        nc.gpsimd.memset(r8s_i, 0)
         nc.gpsimd.memset(b_rows[:], 0.0)
+        nc.vector.memset(r8s_i, 0)
 
         def load_x(g, t, c0, c1):
             nc.sync.dma_start(
@@ -69,30 +69,26 @@ def tile_mix_resid_fm_silu_kernel(tc, x, w4_words, w4_scales, r8_words, r8_scale
         def load_r8(g):
             nc.sync.dma_start(out=r8[g][:].bitcast(I32), in_=r8_words[g].rearrange("p n i -> p (n i)").bitcast(I32))
 
-        def load_scales(queue, view, scales, q):
-            queue.dma_start(
-                out=view[32 * q : 32 * q + 4, :].rearrange("p (g n) -> p g n", g=G),
-                in_=scales.bitcast(I32)[:, 4 * q : 4 * q + 4, :].rearrange("g r n -> r g n"),
-            )
-
         load_x(0, 0, 0, HALF)
         load_x(0, 0, HALF, TW)
-        for q in range(4):
-            load_scales(nc.scalar, w4s_i, w4_scales, q)
-        nc.scalar.activation(out=warm_out[:], in_=warm[:], func=ACT.Silu)
+        def load_scales(view, scales):
+            rows = scales.bitcast(I32).rearrange("g (q r) n -> r q g n", r=4)
+            for r in range(4):
+                nc.sync.dma_start(out=view[r:P:32, :].rearrange("p (g n) -> p g n", g=G), in_=rows[r])
+
+        load_scales(w4s_i, w4_scales)
         load_w4(0)
-        for q in range(4):
-            load_scales(nc.sync, r8s_i, r8_scales, q)
         load_r8(0)
+        load_scales(r8s_i, r8_scales)
+        for q in range(4):
+            nc.gpsimd.dma_start(
+                out=b_rows[32 * q : 32 * q + 8, :],
+                in_=b.rearrange("(m q j) -> q m j", q=4, j=32)[q],
+            )
+        nc.scalar.activation(out=warm_out[:], in_=warm[:], func=ACT.Silu)
         for g in range(1, G):
             load_x(g, 0, 0, TW)
             load_w4(g)
-            if g == 1:
-                for q in range(4):
-                    nc.sync.dma_start(
-                        out=b_rows[32 * q : 32 * q + 8, :],
-                        in_=b.rearrange("(m q j) -> q m j", q=4, j=32)[q],
-                    )
             load_r8(g)
         for t in range(1, NT):
             for g in range(G):
@@ -144,14 +140,15 @@ def tile_mix_resid_fm_silu_kernel(tc, x, w4_words, w4_scales, r8_words, r8_scale
                 stop=(g == G - 1),
             )
 
-        def finish(m, t, c0=0, width=TW):
+        def finish(m, t):
             res = outs.tile([P, TW], F32, name="res")
-            nc.scalar.activation(
-                out=res[:, :width], in_=acc[m][:, :width], func=ACT.Silu, bias=b_cols[:, m : m + 1]
-            )
-            nc.sync.dma_start(
-                out=out[P * m : P * (m + 1), TW * t + c0 : TW * t + c0 + width], in_=res[:, :width]
-            )
+            width = HALF if (t == NT - 1 and m == MT - 1) else TW
+            for c0 in range(0, TW, width):
+                cols = slice(c0, c0 + width)
+                nc.scalar.activation(out=res[:, cols], in_=acc[m][:, cols], func=ACT.Silu, bias=b_cols[:, m : m + 1])
+                nc.sync.dma_start(
+                    out=out[P * m : P * (m + 1), TW * t + c0 : TW * t + c0 + width], in_=res[:, cols]
+                )
 
         def chunk(g, t, width, v_cols):
             parts = [(c0, cast(g, t, c0, width, v_cols)) for c0 in range(0, TW, width)]
@@ -171,15 +168,15 @@ def tile_mix_resid_fm_silu_kernel(tc, x, w4_words, w4_scales, r8_words, r8_scale
 
         for g in range(1, G):
             chunk(g, 0, HALF, V_COLS)
-            if g == 2:
-                nc.vector.transpose(out=b_cols[:], in_=b_rows[:])
+        chunk(0, 1, HALF, HALF)
+        nc.vector.transpose(out=b_cols[:], in_=b_rows[:])
+        for g in range(1, G):
             for m in range(MT):
                 mm_w4(m, g, 0)
                 mm_r8(m, g, 0)
                 if g == G - 1:
                     finish(m, 0)
-
-        for g in range(G):
+        for g in range(1, G):
             chunk(g, 1, HALF, HALF)
         for g in range(G):
             chunk(g, 2, HALF, HALF)
@@ -190,9 +187,7 @@ def tile_mix_resid_fm_silu_kernel(tc, x, w4_words, w4_scales, r8_words, r8_scale
                 if g == G - 1:
                     finish(m, 1)
         for m in range(MT):
-            width = 128 if m == MT - 1 else TW
-            for c0 in range(0, TW, width):
-                for g in range(G):
-                    mm_w4(m, g, 2, c0, width)
-                    mm_r8(m, g, 2, c0, width)
-                finish(m, 2, c0, width)
+            for g in range(G):
+                mm_w4(m, g, 2)
+                mm_r8(m, g, 2)
+            finish(m, 2)

from contextlib import ExitStack

import concourse.mybir as mybir

K, M, T = 1536, 1024, 1536
FLOPS = 2 * 2 * K * M * T

F32 = mybir.dt.float32
BF16 = mybir.dt.bfloat16
I32 = mybir.dt.int32
U32 = mybir.dt.uint32
U8 = mybir.dt.uint8
FP8X4 = mybir.dt.float8_e4m3fn_x4
FP4X4 = mybir.dt.float4_e2m1fn_x4
ACT = mybir.ActivationFunctionType

P = 128
PACK = 4
G = K // 512
MT = M // 128
TW = 512
NT = T // TW
HALF = 256
V_COLS = 160


def tile_mix_resid_fm_silu_kernel(tc, x, w4_words, w4_scales, r8_words, r8_scales, b, out):
    nc = tc.nc
    with ExitStack() as ctx:
        keep = ctx.enter_context(tc.tile_pool(name="keep", bufs=1))
        stage = ctx.enter_context(tc.tile_pool(name="stage", bufs=6))
        outs = ctx.enter_context(tc.tile_pool(name="outs", bufs=26))
        psum = ctx.enter_context(tc.psum_pool(name="psum", bufs=1))
        ctx.enter_context(tc.manual_schedule())

        raw = {}
        codes = {}
        planes = {}
        for t in range(NT):
            for g in range(G):
                raw[g, t] = keep.tile([P, PACK, TW], F32, name="raw_%d_%d" % (g, t), align_bytes=64)
                codes[g, t] = keep.tile([P, TW], U32, name="codes_%d_%d" % (g, t), align_bytes=256)
                planes[g, t] = keep.tile([P, TW], U8, name="plane_%d_%d" % (g, t), align_bytes=256)
        w4 = [keep.tile([P, 2 * M], U8, name="w4_%d" % g, align_bytes=256) for g in range(G)]
        r8 = [keep.tile([P, 4 * M], U8, name="r8_%d" % g, align_bytes=256) for g in range(G)]
        w4s = keep.tile([P, G, M], U8, name="w4s", align_bytes=256)
        r8s = keep.tile([P, G, M], U8, name="r8s", align_bytes=256)
        b_rows = keep.tile([P, 32], F32, name="b_rows", align_bytes=64)
        b_cols = keep.tile([P, 32], F32, name="b_cols", align_bytes=64)
        warm = keep.tile([P, 1], F32, name="warm")
        warm_out = keep.tile([P, 1], F32, name="warm_out")

        w4s_i = w4s[:].rearrange("p g n -> p (g n)").bitcast(I32)
        r8s_i = r8s[:].rearrange("p g n -> p (g n)").bitcast(I32)
        nc.vector.memset(w4s_i, 0)
        nc.vector.memset(warm[:], 0.0)
        nc.gpsimd.memset(b_rows[:], 0.0)
        nc.vector.memset(r8s_i, 0)

        def load_x(g, t, c0, c1):
            nc.sync.dma_start(
                out=raw[g, t][:, :, c0:c1],
                in_=x[512 * g : 512 * (g + 1), TW * t + c0 : TW * t + c1].rearrange("(p j) t -> p j t", j=PACK),
            )

        def load_w4(g):
            nc.sync.dma_start(out=w4[g][:].bitcast(I32), in_=w4_words[g].bitcast(I32))

        def load_r8(g):
            nc.sync.dma_start(out=r8[g][:].bitcast(I32), in_=r8_words[g].rearrange("p n i -> p (n i)").bitcast(I32))

        load_x(0, 0, 0, HALF)
        load_x(0, 0, HALF, TW)
        def load_scales(view, scales):
            rows = scales.bitcast(I32).rearrange("g (q r) n -> r q g n", r=4)
            for r in range(4):
                nc.sync.dma_start(out=view[r:P:32, :].rearrange("p (g n) -> p g n", g=G), in_=rows[r])

        load_scales(w4s_i, w4_scales)
        load_w4(0)
        load_r8(0)
        load_scales(r8s_i, r8_scales)
        for q in range(4):
            nc.gpsimd.dma_start(
                out=b_rows[32 * q : 32 * q + 8, :],
                in_=b.rearrange("(m q j) -> q m j", q=4, j=32)[q],
            )
        nc.scalar.activation(out=warm_out[:], in_=warm[:], func=ACT.Silu)
        for g in range(1, G):
            load_x(g, 0, 0, TW)
            load_w4(g)
            load_r8(g)
        for t in range(1, NT):
            for g in range(G):
                load_x(g, t, 0, TW)

        def cast(g, t, c0, width, v_cols):
            grouped = stage.tile([P, HALF, PACK], BF16, name="grouped", align_bytes=64)
            nc.vector.tensor_copy(
                out=grouped[:, :v_cols, :], in_=raw[g, t][:, :, c0 : c0 + v_cols].rearrange("p j w -> p w j")
            )
            if v_cols < width:
                nc.scalar.copy(
                    out=grouped[:, v_cols:width, :],
                    in_=raw[g, t][:, :, c0 + v_cols : c0 + width].rearrange("p j w -> p w j"),
                )
            return grouped

        def quantise(g, t, c0, width, grouped):
            cols = slice(c0, c0 + width)
            nc.vector.quantize_mx(
                out=codes[g, t][:, cols].bitcast(FP8X4),
                scales=planes[g, t][:, cols],
                in_=grouped[:, :width, :].rearrange("p w j -> p (w j)"),
            )

        acc = {}

        def mm_w4(m, g, t, c0=0, width=TW):
            if g == 0:
                acc[m] = psum.tile([P, TW], F32, name="bank%d" % ((m + c0 // P) % MT))
            nc.tensor.matmul_mx(
                out=acc[m][:, :width],
                lhsT=w4[g][:, 256 * m : 256 * (m + 1)].bitcast(FP4X4),
                lhsT_scale=w4s[:, g, P * m : P * (m + 1)],
                rhs=codes[g, t][:, c0 : c0 + width].bitcast(FP8X4),
                rhs_scale=planes[g, t][:, c0 : c0 + width],
                start=(g == 0),
                stop=False,
            )

        def mm_r8(m, g, t, c0=0, width=TW):
            nc.tensor.matmul_mx(
                out=acc[m][:, :width],
                lhsT=r8[g][:, 512 * m : 512 * (m + 1)].bitcast(FP8X4),
                lhsT_scale=r8s[:, g, P * m : P * (m + 1)],
                rhs=codes[g, t][:, c0 : c0 + width].bitcast(FP8X4),
                rhs_scale=planes[g, t][:, c0 : c0 + width],
                start=False,
                stop=(g == G - 1),
            )

        def finish(m, t):
            res = outs.tile([P, TW], F32, name="res")
            width = HALF if (t == NT - 1 and m == MT - 1) else TW
            for c0 in range(0, TW, width):
                cols = slice(c0, c0 + width)
                nc.scalar.activation(out=res[:, cols], in_=acc[m][:, cols], func=ACT.Silu, bias=b_cols[:, m : m + 1])
                nc.sync.dma_start(
                    out=out[P * m : P * (m + 1), TW * t + c0 : TW * t + c0 + width], in_=res[:, cols]
                )

        def chunk(g, t, width, v_cols):
            parts = [(c0, cast(g, t, c0, width, v_cols)) for c0 in range(0, TW, width)]
            for c0, grouped in parts:
                quantise(g, t, c0, width, grouped)

        halves0 = cast(0, 0, 0, HALF, V_COLS)
        quantise(0, 0, 0, HALF, halves0)
        halves1 = cast(0, 0, 256, 128, 80)
        halves2 = cast(0, 0, 384, 128, 80)
        quantise(0, 0, 256, 128, halves1)
        quantise(0, 0, 384, 128, halves2)
        for m in range(MT):
            mm_w4(m, 0, 0)
        for m in range(MT):
            mm_r8(m, 0, 0)

        for g in range(1, G):
            chunk(g, 0, HALF, V_COLS)
        chunk(0, 1, HALF, HALF)
        nc.vector.transpose(out=b_cols[:], in_=b_rows[:])
        for g in range(1, G):
            for m in range(MT):
                mm_w4(m, g, 0)
                mm_r8(m, g, 0)
                if g == G - 1:
                    finish(m, 0)
        for g in range(1, G):
            chunk(g, 1, HALF, HALF)
        for g in range(G):
            chunk(g, 2, HALF, HALF)
        for g in range(G):
            for m in range(MT):
                mm_w4(m, g, 1)
                mm_r8(m, g, 1)
                if g == G - 1:
                    finish(m, 1)
        for m in range(MT):
            for g in range(G):
                mm_w4(m, g, 2)
                mm_r8(m, g, 2)
            finish(m, 2)
